import numpy as np
import ml_dtypes


def mxq(x, axis, fmt="e4m3"):
    dtype, down = {"e4m3": (ml_dtypes.float8_e4m3fn, 7), "e5m2": (ml_dtypes.float8_e5m2, 14)}[fmt]
    v = np.moveaxis(np.asarray(x, np.float32).astype(ml_dtypes.bfloat16).astype(np.float64), axis, -1)
    blocks = v.reshape(v.shape[:-1] + (-1, 32))
    amax = np.abs(blocks).max(-1, keepdims=True)
    byte = np.maximum(np.where(amax > 0, np.frexp(amax)[1] - 1 + 127, 0) - down, 1)
    scale = np.exp2(byte - 127.0)
    codes = (blocks / scale).astype(np.float32).astype(dtype).astype(np.float64)
    return np.moveaxis((codes * scale).reshape(v.shape), -1, axis)


WIDE = False


def mx_kscale(k):
    if not WIDE:
        return np.ones(k)
    levels = np.array([10, -10, 5, -5, 0])
    if k % 512:
        return np.exp2(np.random.permutation(np.resize(levels, k // 32))).repeat(32)
    a = np.empty((k // 512, 16))
    for p in range(k // 512):
        a[p, :8] = np.random.permutation(np.resize(levels, 8))
        for g in range(8):
            far = levels[np.abs(levels - a[p, g]) >= 10]
            a[p, g + 8] = far[np.random.randint(len(far))]
    return np.exp2(a.ravel()).repeat(32)


def f64(x):
    return np.asarray(x).astype(np.float64)


def striped(idx):
    return np.tile(idx.reshape(-1, 16).T, (8, 1)).astype(np.uint16)


def unstriped(offs):
    return offs[:16].T.reshape(-1).astype(np.int64)


E2M1 = np.array([0.0, 0.5, 1.0, 1.5, 2.0, 3.0, 4.0, 6.0, -0.0, -0.5, -1.0, -1.5, -2.0, -3.0, -4.0, -6.0])


def pack_weight(w, fmt):
    k, n = w.shape
    w = f64(np.asarray(w, np.float32).astype(ml_dtypes.bfloat16)).reshape(k // 32, 32, n)
    amax = np.abs(w).max(1)
    if fmt == "e4m3":
        byte = np.frexp(amax)[1] - 1 + 127 - 7
    else:
        mant, ex = np.frexp(amax / 6.0)
        byte = np.where(mant > 0.5, ex, ex - 1) + 127
    byte = np.clip(np.where(amax > 0, byte, 1), 1, 254)
    scaled = (w * np.exp2(127.0 - byte)[:, None, :]).reshape(k, n).astype(np.float32)
    by_word = np.ascontiguousarray(scaled.reshape(k // 512, 128, 4, n).transpose(0, 1, 3, 2))
    if fmt == "e4m3":
        words = by_word.astype(ml_dtypes.float8_e4m3fn).view(np.uint8)
    else:
        c = by_word.astype(ml_dtypes.float4_e2m1fn).view(np.uint8) & 0xF
        words = (c[..., 0::2] | (c[..., 1::2] << 4)).reshape(k // 512, 128, 2 * n)
    return np.ascontiguousarray(words), np.ascontiguousarray(byte.astype(np.uint8).reshape(k // 512, 16, n))


def unpack_weight(words, scales, fmt):
    g, _, n = scales.shape
    words = np.ascontiguousarray(words).reshape(g, 128, n, -1)
    if fmt == "e4m3":
        vals = words.view(ml_dtypes.float8_e4m3fn).astype(np.float64)
    else:
        nib = np.empty((g, 128, n, 4), np.uint8)
        nib[..., 0::2] = words & 0xF
        nib[..., 1::2] = words >> 4
        vals = E2M1[nib]
    vals = vals * np.repeat(np.exp2(scales.astype(np.float64) - 127.0), 8, axis=1)[..., None]
    return vals.transpose(0, 1, 3, 2).reshape(g * 512, n)


def gelu(v):
    return 0.5 * v * (1.0 + np.tanh(np.sqrt(2.0 / np.pi) * (v + 0.044715 * v**3)))


K, T, S, H, T2, P, N = 1024, 2048, 1024, 512, 2048, 512, 512

def setup_inputs():
    n = np.random.standard_normal
    s = mx_kscale(K)[:, None]
    u = mx_kscale(H)[:, None]
    tab_words, tab_scales = pack_weight(n((K, T)) * s, "e4m3")
    w4_words, w4_scales = pack_weight(n((K, H)) / np.sqrt(K) / s, "e2m1")
    perm = np.random.permutation(T2)
    return {
        "tab_words": tab_words, "tab_scales": tab_scales,
        "offs": striped(np.random.permutation(T)[:S]),
        "w1": (n((K, H)) / np.sqrt(K) / s).astype(np.float32),
        "w4_words": w4_words, "w4_scales": w4_scales,
        "gain": (0.6 * np.exp(0.3 * n(H)) * u[:, 0]).astype(np.float32),
        "page0": (n((H, T2)) * u).astype(np.float32),
        "wgs": np.exp(0.3 * n((128, S))).astype(np.float32),
        "offs2": striped(np.random.permutation(T2)[:S]),
        "offs3": striped(perm[:P]),
        "offs4": striped(perm[P:2 * P]),
        "trade": np.exp(0.4 * n(H)).astype(np.float32),
        "w2": (n((H, N)) / np.sqrt(H) / u).astype(np.float32),
    }

def reference(tab_words, tab_scales, offs, w1, w4_words, w4_scales, gain, page0, wgs, offs2, offs3, offs4, trade, w2):
    v = unpack_weight(tab_words, tab_scales, "e4m3")[:, unstriped(offs)]
    f = mxq(f64(w1), 0, "e4m3").T @ v
    d = unpack_weight(w4_words, w4_scales, "e2m1").T @ v
    h = f64(gain)[:, None] * (np.maximum(f, d) + f)
    page = f64(page0).copy()
    page[:, unstriped(offs2)] = np.tile(f64(wgs), (H // 128, 1)) * h
    a = page[:, unstriped(offs3)]
    b = page[:, unstriped(offs4)]
    page[:, unstriped(offs3)] = a + b
    page[:, unstriped(offs4)] = np.maximum(a, f64(trade)[:, None] * b)
    x = mxq(page, 0, "e4m3")
    return np.tanh(mxq(f64(w2), 0, "e4m3").T @ x)

@@ -1,0 +1,251 @@
+from contextlib import ExitStack
+
+import concourse.mybir as mybir
+from concourse.masks import make_identity
+
+K, T, S, H, T2, PAIRS, N = 1024, 2048, 1024, 512, 2048, 512, 512
+FLOPS = 2 * (2 * K * H * S + H * N * T2)
+
+F32 = mybir.dt.float32
+BF16 = mybir.dt.bfloat16
+I32 = mybir.dt.int32
+U32 = mybir.dt.uint32
+U16 = mybir.dt.uint16
+U8 = mybir.dt.uint8
+FP8X4 = mybir.dt.float8_e4m3fn_x4
+FP4X4 = mybir.dt.float4_e2m1fn_x4
+ALU = mybir.AluOpType
+ACT = mybir.ActivationFunctionType
+
+P = 128
+PACK = 4
+K_PASS = P * PACK
+PASSES = K // K_PASS
+BANK = 512
+QUADRANTS = 4
+LANES = 16
+BLOCKS = S // P
+BOARD_WIDTHS = (256, 256, 512, 512, 512)
+
+
+def interleave(copy, grouped, planes):
+    copy(
+        grouped.rearrange("p (c e) i -> p c i e", e=4),
+        planes.rearrange("p i (c e) -> p c i e", e=4),
+    )
+
+
+def tile_list_seat_trade_board_kernel(
+    tc, tab_words, tab_scales, offs, w1, w4_words, w4_scales, gain, page0, wgs, offs2, offs3, offs4, trade, w2, out
+):
+    nc = tc.nc
+    with ExitStack() as ctx:
+        lists = ctx.enter_context(tc.tile_pool(name="lists", bufs=1))
+        keep = ctx.enter_context(tc.tile_pool(name="keep", bufs=1))
+        ring = ctx.enter_context(tc.tile_pool(name="ring", bufs=2))
+        psum = ctx.enter_context(tc.psum_pool(name="psum", bufs=1))
+
+        def load_list(name, src):
+            tile = lists.tile(list(src.shape), U16, name=name)
+            nc.sync.dma_start(tile[:], src)
+            return tile
+
+        def load_scale_rows(tile, src):
+            for q in range(QUADRANTS):
+                nc.sync.dma_start(
+                    tile[32 * q : 32 * q + 4, :].bitcast(I32).rearrange("p (a w) -> p a w", a=PASSES),
+                    src[:, 4 * q : 4 * q + 4, :].bitcast(I32).rearrange("a r w -> r a w"),
+                )
+
+        def load_weight_rows(rows):
+            raw = ring.tile([P, PACK, rows.shape[1]], F32, name="w_raw")
+            nc.sync.dma_start(raw[:], rows.rearrange("(p i) c -> p i c", i=PACK))
+            return raw
+
+        def quantize_weight(name, raw):
+            width = raw.shape[2]
+            grouped = ring.tile([P, width, PACK], BF16, name="w_grouped", align_bytes=64)
+            codes = keep.tile([P, width], U32, name=name + "_codes", align_bytes=64)
+            scales = keep.tile([P, width], U8, name=name + "_scales", align_bytes=64)
+            interleave(nc.scalar.copy, grouped[:], raw[:])
+            nc.vector.quantize_mx(codes[:].bitcast(FP8X4), scales[:], grouped[:].rearrange("p c i -> p (c i)"))
+            return codes, scales
+
+        wgs_rows = keep.tile([P, PACK, S], F32)
+
+        def load_wgs(t, cols):
+            for q in range(QUADRANTS):
+                nc.sync.dma_start(
+                    wgs_rows[32 * q : 32 * q + 32, t, cols], wgs.rearrange("(m t) j -> t m j", t=PACK)[t, :, cols]
+                )
+
+        def load_page(t):
+            tile = keep.tile([P, T2], F32, name="page%d" % t)
+            nc.sync.dma_start(tile[:], page0.rearrange("(p t) c -> t p c", t=PACK)[t])
+            return tile
+
+        table_scales = keep.tile([P, PASSES * T], U8, align_bytes=64)
+        w4_plane = keep.tile([P, PASSES * H], U8, align_bytes=64)
+        nc.vector.memset(table_scales[:].bitcast(I32), 0)
+        nc.gpsimd.memset(w4_plane[:].bitcast(I32), 0)
+        w1_raw = [load_weight_rows(w1[:K_PASS, :])]
+        idx = load_list("idx", offs)
+        load_scale_rows(table_scales, tab_scales)
+        w1_raw.append(load_weight_rows(w1[K_PASS:, :]))
+
+        def load_table(a):
+            words = keep.tile([P, T], U32, name="table%d" % a)
+            nc.sync.dma_start(words[:].bitcast(I32), tab_words[a].rearrange("p t i -> p (t i)").bitcast(I32))
+            return words
+
+        table = [load_table(0)]
+        w4_codes = keep.tile([P, PASSES * 2 * H], U8, align_bytes=64)
+        nc.sync.dma_start(
+            w4_codes[:].bitcast(I32).rearrange("p (a w) -> p a w", a=PASSES),
+            w4_words.bitcast(I32).rearrange("a p w -> p a w"),
+        )
+        load_scale_rows(w4_plane, w4_scales)
+        table.append(load_table(1))
+        pages = [load_page(0)]
+        gains = keep.tile([P, PACK], F32)
+        nc.sync.dma_start(gains[:], gain.rearrange("(p t) -> p t", t=PACK))
+        idx2 = load_list("idx2", offs2)
+        load_wgs(0, slice(0, BANK))
+        load_wgs(0, slice(BANK, S))
+        idx3 = load_list("idx3", offs3)
+        idx4 = load_list("idx4", offs4)
+        trades = keep.tile([P, PACK], F32)
+        nc.sync.dma_start(trades[:], trade.rearrange("(p t) -> p t", t=PACK))
+        for t in range(1, PACK):
+            load_wgs(t, slice(0, S))
+            pages.append(load_page(t))
+
+        ident = keep.tile([P, P], F32)
+        make_identity(nc, ident[:])
+
+        v_codes = [keep.tile([P, S], U32, name="v_codes%d" % a, align_bytes=64) for a in range(PASSES)]
+        v_scales = [keep.tile([P, S], U8, name="v_scales%d" % a, align_bytes=64) for a in range(PASSES)]
+
+        def entries(tile, cols):
+            return tile[:, cols.start // LANES : cols.stop // LANES]
+
+        def pick_words(a, cols):
+            nc.vector.tensor_copy(v_codes[a][:, cols], table[a][:].indirect(entries(idx, cols)))
+
+        def pick_scales(a, cols):
+            nc.vector.tensor_copy(v_scales[a][:, cols], table_scales[:, a * T : (a + 1) * T].indirect(entries(idx, cols)))
+
+        quarter = S // 4
+        quarters = [slice(q * quarter, (q + 1) * quarter) for q in range(4)]
+        halves = [slice(0, BANK), slice(BANK, S)]
+        for a in range(PASSES):
+            pick_scales(a, halves[0])
+        w1_q = [quantize_weight("w1_0", w1_raw[0])]
+        pick_words(0, halves[0])
+        w1_q.append(quantize_weight("w1_1", w1_raw[1]))
+
+        f_rows = keep.tile([P, BLOCKS, PACK, P], F32, tag="f_then_planes", align_bytes=64)
+        m_rows = keep.tile([P, BLOCKS, PACK, P], F32)
+        h = [keep.tile([P, S], F32, name="h%d" % t) for t in range(PACK)]
+
+        def products(b):
+            cols = slice(b * P, (b + 1) * P)
+            f_bank = psum.tile([P, BANK], F32, tag="mx", bufs=6, name="f_bank")
+            d_bank = psum.tile([P, BANK], F32, tag="mx", bufs=6, name="d_bank")
+            for a in range(PASSES):
+                flags = dict(start=(a == 0), stop=(a == PASSES - 1))
+                picked = dict(lhsT=v_codes[a][:, cols].bitcast(FP8X4), lhsT_scale=v_scales[a][:, cols])
+                nc.tensor.matmul_mx(
+                    f_bank[:], rhs=w1_q[a][0][:].bitcast(FP8X4), rhs_scale=w1_q[a][1][:], **picked, **flags
+                )
+                nc.tensor.matmul_mx(
+                    d_bank[:],
+                    rhs=w4_codes[:, a * 2 * H : (a + 1) * 2 * H].bitcast(FP4X4),
+                    rhs_scale=w4_plane[:, a * H : (a + 1) * H],
+                    **picked,
+                    **flags,
+                )
+            nc.scalar.copy(f_rows[:, b], f_bank[:].rearrange("p (m t) -> p t m", t=PACK))
+            nc.vector.tensor_tensor(
+                m_rows[:, b], d_bank[:].rearrange("p (m t) -> p t m", t=PACK), f_rows[:, b], ALU.max
+            )
+
+        def make_h(t, cols):
+            width = cols.stop - cols.start
+            bank = psum.tile([P, BANK], F32, tag="sum", bufs=2, name="sum_bank")
+            for b in range(cols.start // P, cols.stop // P):
+                at = slice(b * P - cols.start, (b + 1) * P - cols.start)
+                nc.tensor.matmul(bank[:, at], f_rows[:, b, t], ident[:], start=True, stop=False, is_transpose=True)
+                nc.tensor.matmul(bank[:, at], m_rows[:, b, t], ident[:], start=False, stop=True, is_transpose=True)
+            nc.scalar.activation(h[t][:, cols], bank[:, :width], ACT.Copy, scale=gains[:, t : t + 1])
+
+        def write_records(t, cols):
+            nc.vector.tensor_tensor(
+                pages[t][:].indirect(entries(idx2, cols)), h[t][:, cols], wgs_rows[:, t, cols], ALU.mult
+            )
+
+        pick_words(1, quarters[0])
+        pick_words(1, quarters[1])
+        for q, cols in enumerate(quarters):
+            products(2 * q)
+            products(2 * q + 1)
+            if q == 0:
+                for a in range(PASSES):
+                    pick_scales(a, halves[1])
+                    pick_words(a, halves[1])
+            make_h(0, cols)
+            write_records(0, cols)
+        for t in range(1, PACK):
+            for cols in halves:
+                make_h(t, cols)
+
+        w2_codes, w2_scales = quantize_weight("w2", load_weight_rows(w2))
+
+        planes = keep.tile([P, PACK, T2], BF16, tag="f_then_planes", align_bytes=64)
+        for t in range(PACK):
+            a_seat = ring.tile([P, PAIRS], F32)
+            b_seat = ring.tile([P, PAIRS], F32)
+            larger = ring.tile([P, PAIRS], F32)
+            nc.vector.tensor_copy(a_seat[:], pages[t][:].indirect(idx3[:]))
+            nc.vector.tensor_copy(b_seat[:], pages[t][:].indirect(idx4[:]))
+            if t + 1 < PACK:
+                write_records(t + 1, halves[0])
+            nc.vector.scalar_tensor_tensor(
+                larger[:], b_seat[:], trades[:, t : t + 1], a_seat[:], ALU.mult, ALU.max
+            )
+            nc.vector.tensor_tensor(pages[t][:].indirect(idx3[:]), a_seat[:], b_seat[:], ALU.add)
+            if t + 1 < PACK:
+                write_records(t + 1, halves[1])
+            nc.vector.tensor_copy(pages[t][:].indirect(idx4[:]), larger[:])
+            if t + 1 < PACK:
+                nc.scalar.copy(planes[:, t, :], pages[t][:])
+
+        start = 0
+        for c, width in enumerate(BOARD_WIDTHS):
+            cols = slice(start, start + width)
+            start = cols.stop
+            nc.scalar.copy(planes[:, PACK - 1, cols], pages[PACK - 1][:, cols])
+            grouped = keep.tile([P, width, PACK], BF16, name="b_grouped%d" % c, align_bytes=64)
+            codes = keep.tile([P, width], U32, name="b_codes%d" % c, align_bytes=64)
+            scales = keep.tile([P, width], U8, name="b_scales%d" % c, align_bytes=64)
+            interleave(nc.vector.tensor_copy, grouped[:], planes[:, :, cols])
+            nc.vector.quantize_mx(codes[:].bitcast(FP8X4), scales[:], grouped[:].rearrange("p c i -> p (c i)"))
+            per_bank = BANK // width
+            for n0 in range(0, N // P, per_bank):
+                bank = psum.tile([P, per_bank, width], F32, tag="mx", bufs=6, name="score_bank")
+                for u in range(per_bank):
+                    n_cols = slice((n0 + u) * P, (n0 + u + 1) * P)
+                    nc.tensor.matmul_mx(
+                        bank[:, u, :],
+                        lhsT=w2_codes[:, n_cols].bitcast(FP8X4),
+                        lhsT_scale=w2_scales[:, n_cols],
+                        rhs=codes[:].bitcast(FP8X4),
+                        rhs_scale=scales[:],
+                        start=True,
+                        stop=True,
+                    )
+                scores = ring.tile([P, per_bank, width], F32, tag="scores", bufs=6, name="scores")
+                nc.scalar.activation(scores[:], bank[:], ACT.Tanh)
+                nc.sync.dma_start(
+                    out.rearrange("(u p) c -> p u c", p=P)[:, n0 : n0 + per_bank, cols], scores[:]
+                )

@@ -62,21 +62,24 @@ def tile_list_seat_trade_board_kernel(
             nc.sync.dma_start(raw[:], rows.rearrange("(p i) c -> p i c", i=PACK))
             return raw
 
-        def quantize_weight(name, raw):
+        def quantize_weight(name, raw, copies):
             width = raw.shape[2]
             grouped = ring.tile([P, width, PACK], BF16, name="w_grouped", align_bytes=64)
             codes = keep.tile([P, width], U32, name=name + "_codes", align_bytes=64)
             scales = keep.tile([P, width], U8, name=name + "_scales", align_bytes=64)
-            interleave(nc.scalar.copy, grouped[:], raw[:])
+            share = width // len(copies)
+            for i, copy in enumerate(copies):
+                cols = slice(i * share, (i + 1) * share)
+                interleave(copy, grouped[:, cols, :], raw[:, :, cols])
             nc.vector.quantize_mx(codes[:].bitcast(FP8X4), scales[:], grouped[:].rearrange("p c i -> p (c i)"))
             return codes, scales
 
         wgs_rows = keep.tile([P, PACK, S], F32)
 
-        def load_wgs(t, cols):
+        def load_wgs(slots, cols):
             for q in range(QUADRANTS):
                 nc.sync.dma_start(
-                    wgs_rows[32 * q : 32 * q + 32, t, cols], wgs.rearrange("(m t) j -> t m j", t=PACK)[t, :, cols]
+                    wgs_rows[32 * q : 32 * q + 32, slots, cols], wgs.rearrange("(m t) j -> m t j", t=PACK)[:, slots, cols]
                 )
 
         def load_page(t):
@@ -84,14 +87,18 @@ def tile_list_seat_trade_board_kernel(
             nc.sync.dma_start(tile[:], page0.rearrange("(p t) c -> t p c", t=PACK)[t])
             return tile
 
-        table_scales = keep.tile([P, PASSES * T], U8, align_bytes=64)
+        table_scales = keep.tile([P, T], U8, align_bytes=64)
         w4_plane = keep.tile([P, PASSES * H], U8, align_bytes=64)
         nc.vector.memset(table_scales[:].bitcast(I32), 0)
         nc.gpsimd.memset(w4_plane[:].bitcast(I32), 0)
         w1_raw = [load_weight_rows(w1[:K_PASS, :])]
         idx = load_list("idx", offs)
-        load_scale_rows(table_scales, tab_scales)
-        w1_raw.append(load_weight_rows(w1[K_PASS:, :]))
+        idx2 = load_list("idx2", offs2)
+        for q in range(QUADRANTS):
+            nc.sync.dma_start(
+                table_scales[32 * q : 32 * q + 4 * PASSES, :].bitcast(I32),
+                tab_scales[:, 4 * q : 4 * q + 4, :].bitcast(I32),
+            )
 
         def load_table(a):
             words = keep.tile([P, T], U32, name="table%d" % a)
@@ -105,26 +112,33 @@ def tile_list_seat_trade_board_kernel(
             w4_words.bitcast(I32).rearrange("a p w -> p a w"),
         )
         load_scale_rows(w4_plane, w4_scales)
+        w1_raw.append(load_weight_rows(w1[K_PASS:, :]))
+        v_scales = keep.tile([P, S], U8, align_bytes=64)
+        v_scales_moved = keep.tile([P, S], U8, align_bytes=64)
+        nc.gpsimd.memset(v_scales_moved[:].bitcast(I32), 0)
+        nc.vector.tensor_copy(v_scales[:], table_scales[:].indirect(idx[:]))
+        live = 3 * 32 + 4
+        nc.sync.dma_start(v_scales_moved[:live, :].bitcast(I32), v_scales[4 : 4 + live, :].bitcast(I32))
         table.append(load_table(1))
         pages = [load_page(0)]
         gains = keep.tile([P, PACK], F32)
         nc.sync.dma_start(gains[:], gain.rearrange("(p t) -> p t", t=PACK))
-        idx2 = load_list("idx2", offs2)
-        load_wgs(0, slice(0, BANK))
-        load_wgs(0, slice(BANK, S))
+        load_wgs(slice(0, 1), slice(0, BANK))
+        pages.append(load_page(1))
+        load_wgs(slice(1, 2), slice(0, BANK))
+        pages.append(load_page(2))
+        load_wgs(slice(2, 4), slice(0, BANK))
+        pages.append(load_page(3))
+        load_wgs(slice(0, 4), slice(BANK, S))
         idx3 = load_list("idx3", offs3)
         idx4 = load_list("idx4", offs4)
         trades = keep.tile([P, PACK], F32)
         nc.sync.dma_start(trades[:], trade.rearrange("(p t) -> p t", t=PACK))
-        for t in range(1, PACK):
-            load_wgs(t, slice(0, S))
-            pages.append(load_page(t))
 
         ident = keep.tile([P, P], F32)
         make_identity(nc, ident[:])
 
         v_codes = [keep.tile([P, S], U32, name="v_codes%d" % a, align_bytes=64) for a in range(PASSES)]
-        v_scales = [keep.tile([P, S], U8, name="v_scales%d" % a, align_bytes=64) for a in range(PASSES)]
 
         def entries(tile, cols):
             return tile[:, cols.start // LANES : cols.stop // LANES]
@@ -132,52 +146,81 @@ def tile_list_seat_trade_board_kernel(
         def pick_words(a, cols):
             nc.vector.tensor_copy(v_codes[a][:, cols], table[a][:].indirect(entries(idx, cols)))
 
-        def pick_scales(a, cols):
-            nc.vector.tensor_copy(v_scales[a][:, cols], table_scales[:, a * T : (a + 1) * T].indirect(entries(idx, cols)))
-
         quarter = S // 4
         quarters = [slice(q * quarter, (q + 1) * quarter) for q in range(4)]
         halves = [slice(0, BANK), slice(BANK, S)]
-        for a in range(PASSES):
-            pick_scales(a, halves[0])
-        w1_q = [quantize_weight("w1_0", w1_raw[0])]
+        w1_q = [quantize_weight("w1_0", w1_raw[0], [nc.scalar.copy])]
         pick_words(0, halves[0])
-        w1_q.append(quantize_weight("w1_1", w1_raw[1]))
+        pick_words(0, halves[1])
+        w1_q.append(quantize_weight("w1_1", w1_raw[1], [nc.scalar.copy, nc.vector.tensor_copy]))
 
         f_rows = keep.tile([P, BLOCKS, PACK, P], F32, tag="f_then_planes", align_bytes=64)
         m_rows = keep.tile([P, BLOCKS, PACK, P], F32)
         h = [keep.tile([P, S], F32, name="h%d" % t) for t in range(PACK)]
 
-        def products(b):
+        def take_bank(number, shape=(P, BANK)):
+            return psum.tile(list(shape), F32, tag="bank%d" % number, name="bank")
+
+        def products(b, f_number, d_number):
             cols = slice(b * P, (b + 1) * P)
-            f_bank = psum.tile([P, BANK], F32, tag="mx", bufs=6, name="f_bank")
-            d_bank = psum.tile([P, BANK], F32, tag="mx", bufs=6, name="d_bank")
+            f_bank = take_bank(f_number)
+            d_bank = take_bank(d_number)
             for a in range(PASSES):
                 flags = dict(start=(a == 0), stop=(a == PASSES - 1))
-                picked = dict(lhsT=v_codes[a][:, cols].bitcast(FP8X4), lhsT_scale=v_scales[a][:, cols])
+                picked = v_codes[a][:, cols].bitcast(FP8X4)
                 nc.tensor.matmul_mx(
-                    f_bank[:], rhs=w1_q[a][0][:].bitcast(FP8X4), rhs_scale=w1_q[a][1][:], **picked, **flags
+                    f_bank[:],
+                    lhsT=picked,
+                    lhsT_scale=v_scales[4 * a :, cols],
+                    rhs=w1_q[a][0][:].bitcast(FP8X4),
+                    rhs_scale=w1_q[a][1][:],
+                    **flags,
                 )
                 nc.tensor.matmul_mx(
                     d_bank[:],
+                    lhsT=picked,
+                    lhsT_scale=(v_scales, v_scales_moved)[a][:, cols],
                     rhs=w4_codes[:, a * 2 * H : (a + 1) * 2 * H].bitcast(FP4X4),
                     rhs_scale=w4_plane[:, a * H : (a + 1) * H],
-                    **picked,
                     **flags,
                 )
             nc.scalar.copy(f_rows[:, b], f_bank[:].rearrange("p (m t) -> p t m", t=PACK))
-            nc.vector.tensor_tensor(
-                m_rows[:, b], d_bank[:].rearrange("p (m t) -> p t m", t=PACK), f_rows[:, b], ALU.max
-            )
+            d_dealt = d_bank[:].rearrange("p (m t) -> p t m", t=PACK)
+            if b < BLOCKS // 2:
+                nc.vector.tensor_tensor(m_rows[:, b], d_dealt, f_rows[:, b], ALU.max)
+            else:
+                nc.scalar.activation(m_rows[:, b], d_dealt, ACT.Copy, scale=-1.0)
 
-        def make_h(t, cols):
+        def add_transposed(dst, terms):
+            for i, term in enumerate(terms):
+                nc.tensor.matmul(dst, term, ident[:], start=(i == 0), stop=(i == len(terms) - 1), is_transpose=True)
+
+        def make_h(t, cols, number):
             width = cols.stop - cols.start
-            bank = psum.tile([P, BANK], F32, tag="sum", bufs=2, name="sum_bank")
+            bank = take_bank(number)
             for b in range(cols.start // P, cols.stop // P):
                 at = slice(b * P - cols.start, (b + 1) * P - cols.start)
-                nc.tensor.matmul(bank[:, at], f_rows[:, b, t], ident[:], start=True, stop=False, is_transpose=True)
-                nc.tensor.matmul(bank[:, at], m_rows[:, b, t], ident[:], start=False, stop=True, is_transpose=True)
+                add_transposed(bank[:, at], [f_rows[:, b, t], m_rows[:, b, t]])
             nc.scalar.activation(h[t][:, cols], bank[:, :width], ACT.Copy, scale=gains[:, t : t + 1])
+
+        def make_h_by_relu(t, cols, numbers):
+            blocks = range(cols.start // P, cols.stop // P)
+            bank = take_bank(numbers[0], (P, len(blocks), P))
+            for i, b in enumerate(blocks):
+                add_transposed(bank[:, i], [f_rows[:, b, t], m_rows[:, b, t]])
+            excess = ring.tile([P, len(blocks), P], F32)
+            nc.scalar.activation(excess[:], bank[:], ACT.Relu, scale=-1.0)
+            bank = take_bank(numbers[1], (P, len(blocks), P))
+            for i, b in enumerate(blocks):
+                add_transposed(bank[:, i], [excess[:, i]])
+            excess_rows = ring.tile([P, len(blocks), P], F32)
+            nc.scalar.copy(excess_rows[:], bank[:])
+            bank = take_bank(numbers[2], (P, len(blocks), P))
+            for i, b in enumerate(blocks):
+                add_transposed(bank[:, i], [f_rows[:, b, t], f_rows[:, b, t], excess_rows[:, i]])
+            nc.scalar.activation(
+                h[t][:, cols], bank[:].rearrange("p b j -> p (b j)"), ACT.Copy, scale=gains[:, t : t + 1]
+            )
 
         def write_records(t, cols):
             nc.vector.tensor_tensor(
@@ -186,45 +229,56 @@ def tile_list_seat_trade_board_kernel(
 
         pick_words(1, quarters[0])
         pick_words(1, quarters[1])
-        for q, cols in enumerate(quarters):
-            products(2 * q)
-            products(2 * q + 1)
-            if q == 0:
-                for a in range(PASSES):
-                    pick_scales(a, halves[1])
-                    pick_words(a, halves[1])
-            make_h(0, cols)
-            write_records(0, cols)
-        for t in range(1, PACK):
-            for cols in halves:
-                make_h(t, cols)
+        pick_words(1, halves[1])
+        products(0, 0, 1)
+        products(1, 2, 3)
+        make_h(0, quarters[0], 6)
+        write_records(0, quarters[0])
+        products(2, 4, 5)
+        products(3, 7, 3)
+        make_h(0, quarters[1], 0)
+        write_records(0, quarters[1])
+        for t, number in ((1, 2), (2, 4), (3, 1)):
+            make_h(t, halves[0], number)
+            write_records(t, halves[0])
+        for b, numbers in zip(range(BLOCKS // 2, BLOCKS), ((5, 6), (3, 7), (0, 5), (6, 3))):
+            products(b, *numbers)
+        for t in range(PACK):
+            make_h_by_relu(t, halves[1], [(3 * t + i) % 8 for i in range(3)])
 
-        w2_codes, w2_scales = quantize_weight("w2", load_weight_rows(w2))
+        w2_codes, w2_scales = quantize_weight("w2", load_weight_rows(w2), [nc.scalar.copy])
 
         planes = keep.tile([P, PACK, T2], BF16, tag="f_then_planes", align_bytes=64)
-        for t in range(PACK):
-            a_seat = ring.tile([P, PAIRS], F32)
-            b_seat = ring.tile([P, PAIRS], F32)
-            larger = ring.tile([P, PAIRS], F32)
-            nc.vector.tensor_copy(a_seat[:], pages[t][:].indirect(idx3[:]))
-            nc.vector.tensor_copy(b_seat[:], pages[t][:].indirect(idx4[:]))
-            if t + 1 < PACK:
-                write_records(t + 1, halves[0])
-            nc.vector.scalar_tensor_tensor(
-                larger[:], b_seat[:], trades[:, t : t + 1], a_seat[:], ALU.mult, ALU.max
-            )
-            nc.vector.tensor_tensor(pages[t][:].indirect(idx3[:]), a_seat[:], b_seat[:], ALU.add)
-            if t + 1 < PACK:
-                write_records(t + 1, halves[1])
-            nc.vector.tensor_copy(pages[t][:].indirect(idx4[:]), larger[:])
-            if t + 1 < PACK:
-                nc.scalar.copy(planes[:, t, :], pages[t][:])
+        for pair in ((0, 1), (2, 3)):
+            for t in pair:
+                write_records(t, halves[1])
+            seats = {}
+            for t in pair:
+                a_seat = ring.tile([P, PAIRS], F32)
+                b_seat = ring.tile([P, PAIRS], F32)
+                nc.vector.tensor_copy(a_seat[:], pages[t][:].indirect(idx3[:]))
+                nc.vector.tensor_copy(b_seat[:], pages[t][:].indirect(idx4[:]))
+                seats[t] = (a_seat, b_seat)
+            larger = {}
+            for t in pair:
+                a_seat, b_seat = seats[t]
+                larger[t] = ring.tile([P, PAIRS], F32, name="larger")
+                nc.vector.scalar_tensor_tensor(
+                    larger[t][:], b_seat[:], trades[:, t : t + 1], a_seat[:], ALU.mult, ALU.max
+                )
+                nc.vector.tensor_tensor(pages[t][:].indirect(idx3[:]), a_seat[:], b_seat[:], ALU.add)
+            for t in pair:
+                nc.vector.tensor_copy(pages[t][:].indirect(idx4[:]), larger[t][:])
+                if t + 1 < PACK:
+                    nc.scalar.copy(planes[:, t, :], pages[t][:])
 
         start = 0
+        used = 0
         for c, width in enumerate(BOARD_WIDTHS):
             cols = slice(start, start + width)
             start = cols.stop
-            nc.scalar.copy(planes[:, PACK - 1, cols], pages[PACK - 1][:, cols])
+            to_bf16 = nc.scalar.copy if start <= T2 // 2 else nc.vector.tensor_copy
+            to_bf16(planes[:, PACK - 1, cols], pages[PACK - 1][:, cols])
             grouped = keep.tile([P, width, PACK], BF16, name="b_grouped%d" % c, align_bytes=64)
             codes = keep.tile([P, width], U32, name="b_codes%d" % c, align_bytes=64)
             scales = keep.tile([P, width], U8, name="b_scales%d" % c, align_bytes=64)
@@ -232,7 +286,8 @@ def tile_list_seat_trade_board_kernel(
             nc.vector.quantize_mx(codes[:].bitcast(FP8X4), scales[:], grouped[:].rearrange("p c i -> p (c i)"))
             per_bank = BANK // width
             for n0 in range(0, N // P, per_bank):
-                bank = psum.tile([P, per_bank, width], F32, tag="mx", bufs=6, name="score_bank")
+                bank = take_bank(used % 8, (P, per_bank, width))
+                used = used + 1
                 for u in range(per_bank):
                     n_cols = slice((n0 + u) * P, (n0 + u + 1) * P)
                     nc.tensor.matmul_mx(

@@ -76,10 +76,10 @@ def tile_list_seat_trade_board_kernel(
 
         wgs_rows = keep.tile([P, PACK, S], F32)
 
-        def load_wgs(slots, cols):
-            for q in range(QUADRANTS):
+        def load_wgs(t, cols):
+            for q in (0, 2, 1, 3):
                 nc.sync.dma_start(
-                    wgs_rows[32 * q : 32 * q + 32, slots, cols], wgs.rearrange("(m t) j -> m t j", t=PACK)[:, slots, cols]
+                    wgs_rows[32 * q : 32 * q + 32, t, cols], wgs.rearrange("(m t) j -> t m j", t=PACK)[t, :, cols]
                 )
 
         def load_page(t):
@@ -123,17 +123,18 @@ def tile_list_seat_trade_board_kernel(
         pages = [load_page(0)]
         gains = keep.tile([P, PACK], F32)
         nc.sync.dma_start(gains[:], gain.rearrange("(p t) -> p t", t=PACK))
-        load_wgs(slice(0, 1), slice(0, BANK))
-        pages.append(load_page(1))
-        load_wgs(slice(1, 2), slice(0, BANK))
-        pages.append(load_page(2))
-        load_wgs(slice(2, 4), slice(0, BANK))
-        pages.append(load_page(3))
-        load_wgs(slice(0, 4), slice(BANK, S))
+        load_wgs(0, slice(0, BANK))
+        for t in range(1, PACK):
+            pages.append(load_page(t))
+            load_wgs(t, slice(0, BANK))
+        load_wgs(0, slice(BANK, S))
+        load_wgs(1, slice(BANK, S))
         idx3 = load_list("idx3", offs3)
         idx4 = load_list("idx4", offs4)
         trades = keep.tile([P, PACK], F32)
         nc.sync.dma_start(trades[:], trade.rearrange("(p t) -> p t", t=PACK))
+        load_wgs(2, slice(BANK, S))
+        load_wgs(3, slice(BANK, S))
 
         ident = keep.tile([P, P], F32)
         make_identity(nc, ident[:])
@@ -184,12 +185,14 @@ def tile_list_seat_trade_board_kernel(
                     rhs_scale=w4_plane[:, a * H : (a + 1) * H],
                     **flags,
                 )
-            nc.scalar.copy(f_rows[:, b], f_bank[:].rearrange("p (m t) -> p t m", t=PACK))
+            f_dealt = f_bank[:].rearrange("p (m t) -> p t m", t=PACK)
             d_dealt = d_bank[:].rearrange("p (m t) -> p t m", t=PACK)
             if b < BLOCKS // 2:
+                nc.scalar.copy(f_rows[:, b], f_dealt)
                 nc.vector.tensor_tensor(m_rows[:, b], d_dealt, f_rows[:, b], ALU.max)
             else:
-                nc.scalar.activation(m_rows[:, b], d_dealt, ACT.Copy, scale=-1.0)
+                nc.scalar.activation(f_rows[:, b], f_dealt, ACT.Copy, scale=2.0)
+                nc.scalar.activation(m_rows[:, b], d_dealt, ACT.Copy, scale=-2.0)
 
         def add_transposed(dst, terms):
             for i, term in enumerate(terms):
@@ -209,7 +212,7 @@ def tile_list_seat_trade_board_kernel(
             for i, b in enumerate(blocks):
                 add_transposed(bank[:, i], [f_rows[:, b, t], m_rows[:, b, t]])
             excess = ring.tile([P, len(blocks), P], F32)
-            nc.scalar.activation(excess[:], bank[:], ACT.Relu, scale=-1.0)
+            nc.scalar.activation(excess[:], bank[:], ACT.Relu, scale=-0.5)
             bank = take_bank(numbers[1], (P, len(blocks), P))
             for i, b in enumerate(blocks):
                 add_transposed(bank[:, i], [excess[:, i]])
@@ -217,7 +220,7 @@ def tile_list_seat_trade_board_kernel(
             nc.scalar.copy(excess_rows[:], bank[:])
             bank = take_bank(numbers[2], (P, len(blocks), P))
             for i, b in enumerate(blocks):
-                add_transposed(bank[:, i], [f_rows[:, b, t], f_rows[:, b, t], excess_rows[:, i]])
+                add_transposed(bank[:, i], [f_rows[:, b, t], excess_rows[:, i]])
             nc.scalar.activation(
                 h[t][:, cols], bank[:].rearrange("p b j -> p (b j)"), ACT.Copy, scale=gains[:, t : t + 1]
             )

@@ -94,10 +94,10 @@ def tile_list_seat_trade_board_kernel(
         w1_raw = [load_weight_rows(w1[:K_PASS, :])]
         idx = load_list("idx", offs)
         idx2 = load_list("idx2", offs2)
-        for q in range(QUADRANTS):
+        for r in range(4):
             nc.sync.dma_start(
-                table_scales[32 * q : 32 * q + 4 * PASSES, :].bitcast(I32),
-                tab_scales[:, 4 * q : 4 * q + 4, :].bitcast(I32),
+                table_scales[r:P:16, :].bitcast(I32),
+                tab_scales.bitcast(I32).rearrange("a (q r) w -> r q a w", r=4)[r],
             )
 
         def load_table(a):
@@ -118,7 +118,7 @@ def tile_list_seat_trade_board_kernel(
         nc.gpsimd.memset(v_scales_moved[:].bitcast(I32), 0)
         nc.vector.tensor_copy(v_scales[:], table_scales[:].indirect(idx[:]))
         live = 3 * 32 + 4
-        nc.sync.dma_start(v_scales_moved[:live, :].bitcast(I32), v_scales[4 : 4 + live, :].bitcast(I32))
+        nc.sync.dma_start(v_scales_moved[:live, :].bitcast(I32), v_scales[16 : 16 + live, :].bitcast(I32))
         table.append(load_table(1))
         pages = [load_page(0)]
         gains = keep.tile([P, PACK], F32)
@@ -172,7 +172,7 @@ def tile_list_seat_trade_board_kernel(
                 nc.tensor.matmul_mx(
                     f_bank[:],
                     lhsT=picked,
-                    lhsT_scale=v_scales[4 * a :, cols],
+                    lhsT_scale=(v_scales, v_scales_moved)[a][:, cols],
                     rhs=w1_q[a][0][:].bitcast(FP8X4),
                     rhs_scale=w1_q[a][1][:],
                     **flags,
@@ -235,16 +235,16 @@ def tile_list_seat_trade_board_kernel(
         pick_words(1, halves[1])
         products(0, 0, 1)
         products(1, 2, 3)
-        make_h(0, quarters[0], 6)
-        write_records(0, quarters[0])
+        make_h(0, quarters[0], 0)
         products(2, 4, 5)
-        products(3, 7, 3)
-        make_h(0, quarters[1], 0)
+        products(3, 6, 7)
+        make_h(0, quarters[1], 2)
+        write_records(0, quarters[0])
         write_records(0, quarters[1])
-        for t, number in ((1, 2), (2, 4), (3, 1)):
+        for t, number in ((1, 4), (2, 6), (3, 1)):
             make_h(t, halves[0], number)
             write_records(t, halves[0])
-        for b, numbers in zip(range(BLOCKS // 2, BLOCKS), ((5, 6), (3, 7), (0, 5), (6, 3))):
+        for b, numbers in zip(range(BLOCKS // 2, BLOCKS), ((3, 5), (7, 0), (2, 3), (5, 7))):
             products(b, *numbers)
         for t in range(PACK):
             make_h_by_relu(t, halves[1], [(3 * t + i) % 8 for i in range(3)])

from contextlib import ExitStack

import concourse.mybir as mybir
from concourse.masks import make_identity

K, T, S, H, T2, PAIRS, N = 1024, 2048, 1024, 512, 2048, 512, 512
FLOPS = 2 * (2 * K * H * S + H * N * T2)

F32 = mybir.dt.float32
BF16 = mybir.dt.bfloat16
I32 = mybir.dt.int32
U32 = mybir.dt.uint32
U16 = mybir.dt.uint16
U8 = mybir.dt.uint8
FP8X4 = mybir.dt.float8_e4m3fn_x4
FP4X4 = mybir.dt.float4_e2m1fn_x4
ALU = mybir.AluOpType
ACT = mybir.ActivationFunctionType

P = 128
PACK = 4
K_PASS = P * PACK
PASSES = K // K_PASS
BANK = 512
QUADRANTS = 4
LANES = 16
BLOCKS = S // P
BOARD_WIDTHS = (256, 256, 512, 512, 512)


def interleave(copy, grouped, planes):
    copy(
        grouped.rearrange("p (c e) i -> p c i e", e=4),
        planes.rearrange("p i (c e) -> p c i e", e=4),
    )


def tile_list_seat_trade_board_kernel(
    tc, tab_words, tab_scales, offs, w1, w4_words, w4_scales, gain, page0, wgs, offs2, offs3, offs4, trade, w2, out
):
    nc = tc.nc
    with ExitStack() as ctx:
        lists = ctx.enter_context(tc.tile_pool(name="lists", bufs=1))
        keep = ctx.enter_context(tc.tile_pool(name="keep", bufs=1))
        ring = ctx.enter_context(tc.tile_pool(name="ring", bufs=2))
        psum = ctx.enter_context(tc.psum_pool(name="psum", bufs=1))

        def load_list(name, src):
            tile = lists.tile(list(src.shape), U16, name=name)
            nc.sync.dma_start(tile[:], src)
            return tile

        def load_scale_rows(tile, src):
            for q in range(QUADRANTS):
                nc.sync.dma_start(
                    tile[32 * q : 32 * q + 4, :].bitcast(I32).rearrange("p (a w) -> p a w", a=PASSES),
                    src[:, 4 * q : 4 * q + 4, :].bitcast(I32).rearrange("a r w -> r a w"),
                )

        def load_weight_rows(rows):
            raw = ring.tile([P, PACK, rows.shape[1]], F32, name="w_raw")
            nc.sync.dma_start(raw[:], rows.rearrange("(p i) c -> p i c", i=PACK))
            return raw

        def quantize_weight(name, raw, copies):
            width = raw.shape[2]
            grouped = ring.tile([P, width, PACK], BF16, name="w_grouped", align_bytes=64)
            codes = keep.tile([P, width], U32, name=name + "_codes", align_bytes=64)
            scales = keep.tile([P, width], U8, name=name + "_scales", align_bytes=64)
            share = width // len(copies)
            for i, copy in enumerate(copies):
                cols = slice(i * share, (i + 1) * share)
                interleave(copy, grouped[:, cols, :], raw[:, :, cols])
            nc.vector.quantize_mx(codes[:].bitcast(FP8X4), scales[:], grouped[:].rearrange("p c i -> p (c i)"))
            return codes, scales

        wgs_rows = keep.tile([P, PACK, S], F32)

        def load_wgs(t, cols):
            for q in (0, 2, 1, 3):
                nc.sync.dma_start(
                    wgs_rows[32 * q : 32 * q + 32, t, cols], wgs.rearrange("(m t) j -> t m j", t=PACK)[t, :, cols]
                )

        def load_page(t):
            tile = keep.tile([P, T2], F32, name="page%d" % t)
            nc.sync.dma_start(tile[:], page0.rearrange("(p t) c -> t p c", t=PACK)[t])
            return tile

        table_scales = keep.tile([P, T], U8, align_bytes=64)
        w4_plane = keep.tile([P, PASSES * H], U8, align_bytes=64)
        nc.vector.memset(table_scales[:].bitcast(I32), 0)
        nc.gpsimd.memset(w4_plane[:].bitcast(I32), 0)
        w1_raw = [load_weight_rows(w1[:K_PASS, :])]
        idx = load_list("idx", offs)
        idx2 = load_list("idx2", offs2)
        for r in range(4):
            nc.sync.dma_start(
                table_scales[r:P:16, :].bitcast(I32),
                tab_scales.bitcast(I32).rearrange("a (q r) w -> r q a w", r=4)[r],
            )

        def load_table(a):
            words = keep.tile([P, T], U32, name="table%d" % a)
            nc.sync.dma_start(words[:].bitcast(I32), tab_words[a].rearrange("p t i -> p (t i)").bitcast(I32))
            return words

        table = [load_table(0)]
        w4_codes = keep.tile([P, PASSES * 2 * H], U8, align_bytes=64)
        nc.sync.dma_start(
            w4_codes[:].bitcast(I32).rearrange("p (a w) -> p a w", a=PASSES),
            w4_words.bitcast(I32).rearrange("a p w -> p a w"),
        )
        load_scale_rows(w4_plane, w4_scales)
        w1_raw.append(load_weight_rows(w1[K_PASS:, :]))
        v_scales = keep.tile([P, S], U8, align_bytes=64)
        v_scales_moved = keep.tile([P, S], U8, align_bytes=64)
        nc.gpsimd.memset(v_scales_moved[:].bitcast(I32), 0)
        nc.vector.tensor_copy(v_scales[:], table_scales[:].indirect(idx[:]))
        live = 3 * 32 + 4
        nc.sync.dma_start(v_scales_moved[:live, :].bitcast(I32), v_scales[16 : 16 + live, :].bitcast(I32))
        table.append(load_table(1))
        pages = [load_page(0)]
        gains = keep.tile([P, PACK], F32)
        nc.sync.dma_start(gains[:], gain.rearrange("(p t) -> p t", t=PACK))
        load_wgs(0, slice(0, BANK))
        for t in range(1, PACK):
            pages.append(load_page(t))
            load_wgs(t, slice(0, BANK))
        load_wgs(0, slice(BANK, S))
        load_wgs(1, slice(BANK, S))
        idx3 = load_list("idx3", offs3)
        idx4 = load_list("idx4", offs4)
        trades = keep.tile([P, PACK], F32)
        nc.sync.dma_start(trades[:], trade.rearrange("(p t) -> p t", t=PACK))
        load_wgs(2, slice(BANK, S))
        load_wgs(3, slice(BANK, S))

        ident = keep.tile([P, P], F32)
        make_identity(nc, ident[:])

        v_codes = [keep.tile([P, S], U32, name="v_codes%d" % a, align_bytes=64) for a in range(PASSES)]

        def entries(tile, cols):
            return tile[:, cols.start // LANES : cols.stop // LANES]

        def pick_words(a, cols):
            nc.vector.tensor_copy(v_codes[a][:, cols], table[a][:].indirect(entries(idx, cols)))

        quarter = S // 4
        quarters = [slice(q * quarter, (q + 1) * quarter) for q in range(4)]
        halves = [slice(0, BANK), slice(BANK, S)]
        w1_q = [quantize_weight("w1_0", w1_raw[0], [nc.scalar.copy])]
        pick_words(0, halves[0])
        pick_words(0, halves[1])
        w1_q.append(quantize_weight("w1_1", w1_raw[1], [nc.scalar.copy, nc.vector.tensor_copy]))

        f_rows = keep.tile([P, BLOCKS, PACK, P], F32, tag="f_then_planes", align_bytes=64)
        m_rows = keep.tile([P, BLOCKS, PACK, P], F32)
        h = [keep.tile([P, S], F32, name="h%d" % t) for t in range(PACK)]

        def take_bank(number, shape=(P, BANK)):
            return psum.tile(list(shape), F32, tag="bank%d" % number, name="bank")

        def products(b, f_number, d_number):
            cols = slice(b * P, (b + 1) * P)
            f_bank = take_bank(f_number)
            d_bank = take_bank(d_number)
            for a in range(PASSES):
                flags = dict(start=(a == 0), stop=(a == PASSES - 1))
                picked = v_codes[a][:, cols].bitcast(FP8X4)
                nc.tensor.matmul_mx(
                    f_bank[:],
                    lhsT=picked,
                    lhsT_scale=(v_scales, v_scales_moved)[a][:, cols],
                    rhs=w1_q[a][0][:].bitcast(FP8X4),
                    rhs_scale=w1_q[a][1][:],
                    **flags,
                )
                nc.tensor.matmul_mx(
                    d_bank[:],
                    lhsT=picked,
                    lhsT_scale=(v_scales, v_scales_moved)[a][:, cols],
                    rhs=w4_codes[:, a * 2 * H : (a + 1) * 2 * H].bitcast(FP4X4),
                    rhs_scale=w4_plane[:, a * H : (a + 1) * H],
                    **flags,
                )
            f_dealt = f_bank[:].rearrange("p (m t) -> p t m", t=PACK)
            d_dealt = d_bank[:].rearrange("p (m t) -> p t m", t=PACK)
            if b < BLOCKS // 2:
                nc.scalar.copy(f_rows[:, b], f_dealt)
                nc.vector.tensor_tensor(m_rows[:, b], d_dealt, f_rows[:, b], ALU.max)
            else:
                nc.scalar.activation(f_rows[:, b], f_dealt, ACT.Copy, scale=2.0)
                nc.scalar.activation(m_rows[:, b], d_dealt, ACT.Copy, scale=-2.0)

        def add_transposed(dst, terms):
            for i, term in enumerate(terms):
                nc.tensor.matmul(dst, term, ident[:], start=(i == 0), stop=(i == len(terms) - 1), is_transpose=True)

        def make_h(t, cols, number):
            width = cols.stop - cols.start
            bank = take_bank(number)
            for b in range(cols.start // P, cols.stop // P):
                at = slice(b * P - cols.start, (b + 1) * P - cols.start)
                add_transposed(bank[:, at], [f_rows[:, b, t], m_rows[:, b, t]])
            nc.scalar.activation(h[t][:, cols], bank[:, :width], ACT.Copy, scale=gains[:, t : t + 1])

        def make_h_by_relu(t, cols, numbers):
            blocks = range(cols.start // P, cols.stop // P)
            bank = take_bank(numbers[0], (P, len(blocks), P))
            for i, b in enumerate(blocks):
                add_transposed(bank[:, i], [f_rows[:, b, t], m_rows[:, b, t]])
            excess = ring.tile([P, len(blocks), P], F32)
            nc.scalar.activation(excess[:], bank[:], ACT.Relu, scale=-0.5)
            bank = take_bank(numbers[1], (P, len(blocks), P))
            for i, b in enumerate(blocks):
                add_transposed(bank[:, i], [excess[:, i]])
            excess_rows = ring.tile([P, len(blocks), P], F32)
            nc.scalar.copy(excess_rows[:], bank[:])
            bank = take_bank(numbers[2], (P, len(blocks), P))
            for i, b in enumerate(blocks):
                add_transposed(bank[:, i], [f_rows[:, b, t], excess_rows[:, i]])
            nc.scalar.activation(
                h[t][:, cols], bank[:].rearrange("p b j -> p (b j)"), ACT.Copy, scale=gains[:, t : t + 1]
            )

        def write_records(t, cols):
            nc.vector.tensor_tensor(
                pages[t][:].indirect(entries(idx2, cols)), h[t][:, cols], wgs_rows[:, t, cols], ALU.mult
            )

        pick_words(1, quarters[0])
        pick_words(1, quarters[1])
        pick_words(1, halves[1])
        products(0, 0, 1)
        products(1, 2, 3)
        make_h(0, quarters[0], 0)
        products(2, 4, 5)
        products(3, 6, 7)
        make_h(0, quarters[1], 2)
        write_records(0, quarters[0])
        write_records(0, quarters[1])
        for t, number in ((1, 4), (2, 6), (3, 1)):
            make_h(t, halves[0], number)
            write_records(t, halves[0])
        for b, numbers in zip(range(BLOCKS // 2, BLOCKS), ((3, 5), (7, 0), (2, 3), (5, 7))):
            products(b, *numbers)
        for t in range(PACK):
            make_h_by_relu(t, halves[1], [(3 * t + i) % 8 for i in range(3)])

        w2_codes, w2_scales = quantize_weight("w2", load_weight_rows(w2), [nc.scalar.copy])

        planes = keep.tile([P, PACK, T2], BF16, tag="f_then_planes", align_bytes=64)
        for pair in ((0, 1), (2, 3)):
            for t in pair:
                write_records(t, halves[1])
            seats = {}
            for t in pair:
                a_seat = ring.tile([P, PAIRS], F32)
                b_seat = ring.tile([P, PAIRS], F32)
                nc.vector.tensor_copy(a_seat[:], pages[t][:].indirect(idx3[:]))
                nc.vector.tensor_copy(b_seat[:], pages[t][:].indirect(idx4[:]))
                seats[t] = (a_seat, b_seat)
            larger = {}
            for t in pair:
                a_seat, b_seat = seats[t]
                larger[t] = ring.tile([P, PAIRS], F32, name="larger")
                nc.vector.scalar_tensor_tensor(
                    larger[t][:], b_seat[:], trades[:, t : t + 1], a_seat[:], ALU.mult, ALU.max
                )
                nc.vector.tensor_tensor(pages[t][:].indirect(idx3[:]), a_seat[:], b_seat[:], ALU.add)
            for t in pair:
                nc.vector.tensor_copy(pages[t][:].indirect(idx4[:]), larger[t][:])
                if t + 1 < PACK:
                    nc.scalar.copy(planes[:, t, :], pages[t][:])

        start = 0
        used = 0
        for c, width in enumerate(BOARD_WIDTHS):
            cols = slice(start, start + width)
            start = cols.stop
            to_bf16 = nc.scalar.copy if start <= T2 // 2 else nc.vector.tensor_copy
            to_bf16(planes[:, PACK - 1, cols], pages[PACK - 1][:, cols])
            grouped = keep.tile([P, width, PACK], BF16, name="b_grouped%d" % c, align_bytes=64)
            codes = keep.tile([P, width], U32, name="b_codes%d" % c, align_bytes=64)
            scales = keep.tile([P, width], U8, name="b_scales%d" % c, align_bytes=64)
            interleave(nc.vector.tensor_copy, grouped[:], planes[:, :, cols])
            nc.vector.quantize_mx(codes[:].bitcast(FP8X4), scales[:], grouped[:].rearrange("p c i -> p (c i)"))
            per_bank = BANK // width
            for n0 in range(0, N // P, per_bank):
                bank = take_bank(used % 8, (P, per_bank, width))
                used = used + 1
                for u in range(per_bank):
                    n_cols = slice((n0 + u) * P, (n0 + u + 1) * P)
                    nc.tensor.matmul_mx(
                        bank[:, u, :],
                        lhsT=w2_codes[:, n_cols].bitcast(FP8X4),
                        lhsT_scale=w2_scales[:, n_cols],
                        rhs=codes[:].bitcast(FP8X4),
                        rhs_scale=scales[:],
                        start=True,
                        stop=True,
                    )
                scores = ring.tile([P, per_bank, width], F32, tag="scores", bufs=6, name="scores")
                nc.scalar.activation(scores[:], bank[:], ACT.Tanh)
                nc.sync.dma_start(
                    out.rearrange("(u p) c -> p u c", p=P)[:, n0 : n0 + per_bank, cols], scores[:]
                )
